import numpy as np
import ml_dtypes


def mxq(x, axis, fmt="e4m3"):
    dtype, down = {"e4m3": (ml_dtypes.float8_e4m3fn, 7), "e5m2": (ml_dtypes.float8_e5m2, 14)}[fmt]
    v = np.moveaxis(np.asarray(x, np.float32).astype(ml_dtypes.bfloat16).astype(np.float64), axis, -1)
    blocks = v.reshape(v.shape[:-1] + (-1, 32))
    amax = np.abs(blocks).max(-1, keepdims=True)
    byte = np.maximum(np.where(amax > 0, np.frexp(amax)[1] - 1 + 127, 0) - down, 1)
    scale = np.exp2(byte - 127.0)
    codes = (blocks / scale).astype(np.float32).astype(dtype).astype(np.float64)
    return np.moveaxis((codes * scale).reshape(v.shape), -1, axis)


WIDE = False


def mx_kscale(k):
    if not WIDE:
        return np.ones(k)
    levels = np.array([10, -10, 5, -5, 0])
    if k % 512:
        return np.exp2(np.random.permutation(np.resize(levels, k // 32))).repeat(32)
    a = np.empty((k // 512, 16))
    for p in range(k // 512):
        a[p, :8] = np.random.permutation(np.resize(levels, 8))
        for g in range(8):
            far = levels[np.abs(levels - a[p, g]) >= 10]
            a[p, g + 8] = far[np.random.randint(len(far))]
    return np.exp2(a.ravel()).repeat(32)


def f64(x):
    return np.asarray(x).astype(np.float64)


def striped(idx):
    return np.tile(idx.reshape(-1, 16).T, (8, 1)).astype(np.uint16)


def unstriped(offs):
    return offs[:16].T.reshape(-1).astype(np.int64)


E2M1 = np.array([0.0, 0.5, 1.0, 1.5, 2.0, 3.0, 4.0, 6.0, -0.0, -0.5, -1.0, -1.5, -2.0, -3.0, -4.0, -6.0])


def pack_weight(w, fmt):
    k, n = w.shape
    w = f64(np.asarray(w, np.float32).astype(ml_dtypes.bfloat16)).reshape(k // 32, 32, n)
    amax = np.abs(w).max(1)
    if fmt == "e4m3":
        byte = np.frexp(amax)[1] - 1 + 127 - 7
    else:
        mant, ex = np.frexp(amax / 6.0)
        byte = np.where(mant > 0.5, ex, ex - 1) + 127
    byte = np.clip(np.where(amax > 0, byte, 1), 1, 254)
    scaled = (w * np.exp2(127.0 - byte)[:, None, :]).reshape(k, n).astype(np.float32)
    by_word = np.ascontiguousarray(scaled.reshape(k // 512, 128, 4, n).transpose(0, 1, 3, 2))
    if fmt == "e4m3":
        words = by_word.astype(ml_dtypes.float8_e4m3fn).view(np.uint8)
    else:
        c = by_word.astype(ml_dtypes.float4_e2m1fn).view(np.uint8) & 0xF
        words = (c[..., 0::2] | (c[..., 1::2] << 4)).reshape(k // 512, 128, 2 * n)
    return np.ascontiguousarray(words), np.ascontiguousarray(byte.astype(np.uint8).reshape(k // 512, 16, n))


def unpack_weight(words, scales, fmt):
    g, _, n = scales.shape
    words = np.ascontiguousarray(words).reshape(g, 128, n, -1)
    if fmt == "e4m3":
        vals = words.view(ml_dtypes.float8_e4m3fn).astype(np.float64)
    else:
        nib = np.empty((g, 128, n, 4), np.uint8)
        nib[..., 0::2] = words & 0xF
        nib[..., 1::2] = words >> 4
        vals = E2M1[nib]
    vals = vals * np.repeat(np.exp2(scales.astype(np.float64) - 127.0), 8, axis=1)[..., None]
    return vals.transpose(0, 1, 3, 2).reshape(g * 512, n)


def gelu(v):
    return 0.5 * v * (1.0 + np.tanh(np.sqrt(2.0 / np.pi) * (v + 0.044715 * v**3)))


K, KA, KB, H, T, S, T2, P = 1536, 1024, 512, 1024, 4096, 1024, 2048, 512

def setup_inputs():
    n = np.random.standard_normal
    s = mx_kscale(K)[:, None]
    u = mx_kscale(H)
    tab_words, tab_scales = pack_weight(n((K, T)) * s, "e4m3")
    w4_words, w4_scales = pack_weight(1.5 * n((KA, H)) / np.sqrt(K) / s[:KA], "e2m1")
    return {
        "tab_words": tab_words, "tab_scales": tab_scales,
        "offs": striped(np.random.permutation(T)[:S]),
        "offs2": striped(np.random.permutation(T2)[:S]),
        "offs3": striped(np.random.permutation(T2)[:P]),
        "offs4": striped(np.random.permutation(T2)[:P]),
        "w4_words": w4_words, "w4_scales": w4_scales,
        "w1": (1.5 * n((KB, H)) / np.sqrt(K) / s[KA:]).astype(np.float32),
        "b1": (0.6 * n(H)).astype(np.float32),
        "gain": (1.4 * np.exp(0.3 * n(H)) * u).astype(np.float32),
        "wgs": np.exp(0.3 * n((128, S))).astype(np.float32),
        "page0": (n((H, T2)) * u[:, None]).astype(np.float32),
        "dv": (n(H) / np.sqrt(H) / u ** 2).astype(np.float32),
        "fam": n(P).astype(np.float32),
    }

def reference(tab_words, tab_scales, offs, offs2, offs3, offs4, w4_words, w4_scales, w1, b1, gain, wgs, page0, dv, fam):
    v = unpack_weight(tab_words, tab_scales, "e4m3")[:, unstriped(offs)]
    w4 = unpack_weight(w4_words, w4_scales, "e2m1")
    wq = mxq(f64(w1), 0, "e4m3")
    acc = w4.T @ v[:KA] + wq.T @ v[KA:]
    h = np.tanh(acc + f64(b1)[:, None]) * f64(gain)[:, None]
    page = f64(page0).copy()
    page[:, unstriped(offs2)] = np.tile(f64(wgs), (H // 128, 1)) * h
    x1 = page[:, unstriped(offs3)]
    x2 = np.abs(page[:, unstriped(offs4)]) * f64(dv)[:, None]
    e = mxq(x1, 0, "e4m3").T @ mxq(x2, 0, "e4m3")
    return e + f64(fam)[None, :]

@@ -1,0 +1,247 @@
+from contextlib import ExitStack
+
+import concourse.mybir as mybir
+
+FLOPS = 3758096384
+
+F32 = mybir.dt.float32
+BF16 = mybir.dt.bfloat16
+I32 = mybir.dt.int32
+U32 = mybir.dt.uint32
+U16 = mybir.dt.uint16
+U8 = mybir.dt.uint8
+FP8X4 = mybir.dt.float8_e4m3fn_x4
+FP4X4 = mybir.dt.float4_e2m1fn_x4
+ACT = mybir.ActivationFunctionType
+ALU = mybir.AluOpType
+
+P = 128
+T = 4096
+S = 1024
+T2 = 2048
+M = 512
+H = 1024
+HALF = 512
+NT = 8
+
+
+def tile_list_plating_bath_match_kernel(
+    tc, tab_words, tab_scales, offs, offs2, offs3, offs4, w4_words, w4_scales,
+    w1, b1, gain, wgs, page0, dv, fam, out,
+):
+    nc = tc.nc
+    with ExitStack() as ctx:
+        keep = ctx.enter_context(tc.tile_pool(name="keep", bufs=1))
+        ring = ctx.enter_context(tc.tile_pool(name="ring", bufs=2))
+        pages = ctx.enter_context(tc.tile_pool(name="pages", bufs=5))
+        acc_pool = ctx.enter_context(tc.psum_pool(name="acc", bufs=4))
+        e_pool = ctx.enter_context(tc.psum_pool(name="e", bufs=1))
+
+        idx = keep.tile([P, S // 16], U16, name="idx")
+        idx2 = keep.tile([P, S // 16], U16, name="idx2")
+        idx3 = keep.tile([P, M // 16], U16, name="idx3")
+        idx4 = keep.tile([P, M // 16], U16, name="idx4")
+        tab = [keep.tile([P, T], I32, name="tab%d" % a, tag="tab%d" % a, align_bytes=64) for a in range(3)]
+        tab_sc = keep.tile([P, T], U8, name="tab_sc", tag="tab_sc", align_bytes=64)
+        v_words = {}
+        v_sc = keep.tile([P, S], U8, name="v_sc", align_bytes=64)
+        v_sc1 = keep.tile([P, S], U8, name="v_sc1", align_bytes=64)
+        w4_raw = keep.tile([P, 2, 2 * H], U8, name="w4_raw")
+        w4_dealt = keep.tile([P, 2, 2 * H], U8, name="w4_dealt", align_bytes=64)
+        w4s_raw = keep.tile([P, 2, H], U8, name="w4s_raw", tag="w4s_raw", align_bytes=64)
+        w4s_dealt = keep.tile([P, 2, H], U8, name="w4s_dealt", align_bytes=64)
+        b1_sb = keep.tile([P, 2, 4], F32, name="b1_sb")
+        gain_sb = keep.tile([P, 2, 4], F32, name="gain_sb")
+        dv_sb = keep.tile([P, 2, 4], F32, name="dv_sb")
+        fam_sb = keep.tile([P, M], F32, name="fam_sb")
+        wg0 = [keep.tile([P, HALF], F32, name="wg0_%d" % h) for h in range(2)]
+        wg1 = keep.tile([P, S], F32, name="wg1")
+        wg23 = keep.tile([P, 2, S], F32, name="wg23")
+        w1_codes, w1_sc = {}, {}
+        x1_in = [keep.tile([P, M, 4], BF16, name="x1_in%d" % b, align_bytes=64) for b in range(2)]
+        x2_in = [keep.tile([P, M, 4], BF16, name="x2_in%d" % b, align_bytes=64) for b in range(2)]
+        x1_last = keep.tile([P, 2, M], F32, name="x1_last")
+
+        nc.gpsimd.memset(tab_sc[:].bitcast(I32), 0)
+        nc.vector.memset(w4s_raw[:].rearrange("p a c -> p (a c)").bitcast(I32), 0)
+        nc.vector.memset(v_sc1[:].bitcast(I32), 0)
+
+        def load_tab(a):
+            nc.sync.dma_start(out=tab[a][:], in_=tab_words[a].rearrange("p n t -> p (n t)").bitcast(I32))
+
+        def load_w1(b):
+            raw = keep.tile([P, 4, HALF], F32, name="w1_raw%d" % b, tag="w1_raw%d" % b)
+            nc.sync.dma_start(out=raw[:], in_=w1[:, b * HALF:(b + 1) * HALF].rearrange("(p j) c -> p j c", j=4))
+            return raw
+
+        def load_page(i):
+            b, t = divmod(i, 4)
+            page = pages.tile([P, T2], F32, name="page")
+            nc.sync.dma_start(out=page[:], in_=page0[b * HALF:(b + 1) * HALF, :].rearrange("(p t) c -> t p c", t=4)[t])
+            return page
+
+        wgs_rows = wgs.rearrange("(x t) j -> x t j", t=4)
+
+        def load_wg0(h):
+            for u in range(4):
+                nc.sync.dma_start(out=wg0[h][32 * u:32 * u + 32, :], in_=wgs_rows[:, 0, h * HALF:(h + 1) * HALF])
+
+        def load_vec(dst, src):
+            nc.sync.dma_start(out=dst[:], in_=src.rearrange("(b p t) -> p b t", b=2, t=4))
+
+        for q in range(4):
+            nc.gpsimd.dma_start(out=tab_sc[32 * q:32 * q + 12, :].bitcast(I32),
+                                in_=tab_scales[:, 4 * q:4 * q + 4, :].bitcast(I32))
+        for q in range(4):
+            nc.gpsimd.dma_start(out=w4s_raw[32 * q:32 * q + 4, :, :].bitcast(I32),
+                                in_=w4_scales[:, 4 * q:4 * q + 4, :].rearrange("a r c -> r a c").bitcast(I32))
+        nc.sync.dma_start(idx[:], offs)
+        load_tab(0)
+        nc.sync.dma_start(out=w4_raw[:].bitcast(I32), in_=w4_words.rearrange("a p c -> p a c").bitcast(I32))
+        w1_raw0 = load_w1(0)
+        load_tab(1)
+        load_vec(b1_sb, b1)
+        load_tab(2)
+        load_vec(gain_sb, gain)
+        nc.sync.dma_start(idx2[:], offs2)
+        load_wg0(0)
+        page_tiles = [load_page(0)]
+        load_wg0(1)
+
+        def gather_words(a, lo, hi):
+            if a not in v_words:
+                v_words[a] = keep.tile([P, S], U32, name="v_words%d" % a, align_bytes=64,
+                                       tag=("v_words0", "tab_sc", "w1_grouped0")[a])
+            nc.vector.tensor_copy(v_words[a][:, lo:hi], tab[a][:].bitcast(U32).indirect(idx[:, lo // 16:hi // 16]))
+
+        def round_w1(b, raw):
+            grouped = keep.tile([P, 4, P, 4], BF16, name="w1_grouped%d" % b, tag="w1_grouped%d" % b, align_bytes=64)
+            nc.scalar.copy(out=grouped[:].rearrange("p t m j -> p m t j"),
+                           in_=raw[:].rearrange("p j (m t) -> p m t j", t=4))
+            return grouped
+
+        def quantize_w1(b, grouped):
+            w1_codes[b] = keep.tile([P, HALF], U32, name="w1_codes%d" % b, tag=("tab1", "w1_codes1")[b], align_bytes=64)
+            w1_sc[b] = keep.tile([P, HALF], U8, name="w1_sc%d" % b, tag=("w4s_raw", "w1_sc1")[b], align_bytes=64)
+            nc.vector.quantize_mx(out=w1_codes[b][:].bitcast(FP8X4), scales=w1_sc[b][:],
+                                  in_=grouped[:].rearrange("p t m j -> p (t m j)"))
+
+        gather_words(0, 0, S)
+        nc.vector.tensor_copy(v_sc[:], tab_sc[:].indirect(idx[:]))
+        nc.gpsimd.dma_start(out=v_sc1[0:112, :].bitcast(I32), in_=v_sc[4:116, :].bitcast(I32))
+        nc.vector.tensor_copy(
+            out=w4_dealt[:].bitcast(U16).rearrange("p a (b t m) -> p (a b) t m", b=2, t=4),
+            in_=w4_raw[:].bitcast(U16).rearrange("p a (b m t) -> p (a b) t m", b=2, t=4))
+        nc.vector.tensor_copy(
+            out=w4s_dealt[:].rearrange("p a (b t m) -> p (a b) t m", b=2, t=4),
+            in_=w4s_raw[:].rearrange("p a (b m t) -> p (a b) t m", b=2, t=4))
+        gather_words(1, 0, S)
+        quantize_w1(0, round_w1(0, w1_raw0))
+        gather_words(2, 0, HALF)
+        gather_words(2, HALF, S)
+
+        w1_raw1 = load_w1(1)
+        nc.sync.dma_start(idx4[:], offs4)
+        nc.sync.dma_start(idx3[:], offs3)
+        load_vec(dv_sb, dv)
+        for u in range(4):
+            nc.sync.dma_start(out=wg1[32 * u:32 * u + 32, :], in_=wgs_rows[:, 1, :])
+        page_tiles.append(load_page(1))
+        for u in range(4):
+            nc.sync.dma_start(out=wg23[32 * u:32 * u + 32, :, :], in_=wgs_rows[:, 2:4, :])
+        page_tiles.append(load_page(2))
+        page_tiles.append(load_page(3))
+        nc.sync.dma_start(out=fam_sb[:], in_=fam.partition_broadcast(P))
+        for i in range(4, NT):
+            page_tiles.append(load_page(i))
+
+        def first_stage(i):
+            b, t = divmod(i, 4)
+            th = ring.tile([P, S], F32, name="th")
+            if i == 4:
+                gw = keep.tile([P, S], F32, name="gw4", tag="gw4", align_bytes=64)
+            else:
+                gw = ring.tile([P, S], F32, name="gw")
+            for h in range(2):
+                cols = slice(h * HALF, (h + 1) * HALF)
+                if t == 0:
+                    nc.scalar.activation(gw[:, cols], wg0[h][:], ACT.Copy, scale=gain_sb[:, b, t:t + 1])
+                acc = acc_pool.tile([P, HALF], F32, name="acc")
+                for a in range(2):
+                    nc.tensor.matmul_mx(
+                        out=acc[:],
+                        lhsT=w4_dealt[:, a, 2 * P * i:2 * P * (i + 1)].bitcast(FP4X4),
+                        lhsT_scale=w4s_dealt[:, a, P * i:P * (i + 1)],
+                        rhs=v_words[a][:, cols].bitcast(FP8X4),
+                        rhs_scale=(v_sc, v_sc1)[a][:, cols],
+                        start=(a == 0), stop=False)
+                nc.tensor.matmul_mx(
+                    out=acc[:],
+                    lhsT=w1_codes[b][:, P * t:P * (t + 1)].bitcast(FP8X4),
+                    lhsT_scale=w1_sc[b][:, P * t:P * (t + 1)],
+                    rhs=v_words[2][:, cols].bitcast(FP8X4),
+                    rhs_scale=v_sc[8:P, cols],
+                    start=False, stop=True)
+                nc.scalar.activation(th[:, cols], acc[:], ACT.Tanh, bias=b1_sb[:, b, t:t + 1])
+            if t > 0:
+                nc.scalar.activation(gw[:], wg1[:] if t == 1 else wg23[:, t - 2, :], ACT.Copy, scale=gain_sb[:, b, t:t + 1])
+            return th, gw
+
+        def scatter(i, th, gw):
+            pieces = [(0, HALF), (HALF, S)] if i == 0 else [(0, S)]
+            for lo, hi in pieces:
+                nc.vector.tensor_tensor(page_tiles[i][:].indirect(idx2[:, lo // 16:hi // 16]),
+                                        th[:, lo:hi], gw[:, lo:hi], ALU.mult)
+
+        def fetch(i):
+            b, t = divmod(i, 4)
+            page = page_tiles[i]
+            g4 = ring.tile([P, M], F32, name="g4")
+            nc.vector.tensor_copy(g4[:], page[:].indirect(idx4[:]))
+            if i >= NT - 2:
+                nc.vector.tensor_copy(x1_last[:, i - (NT - 2), :], page[:].indirect(idx3[:]))
+            else:
+                g3 = ring.tile([P, M], F32, name="g3")
+                nc.vector.tensor_copy(g3[:], page[:].indirect(idx3[:]))
+            if i == 0:
+                mag = keep.tile([P, M], F32, name="mag0", tag="w1_raw1")
+            else:
+                mag = ring.tile([P, M], F32, name="mag")
+            nc.scalar.activation(mag[:], g4[:], ACT.Abs)
+            nc.scalar.activation(x2_in[b][:, :, t], mag[:], ACT.Copy, scale=dv_sb[:, b, t:t + 1])
+            if i < NT - 2:
+                nc.scalar.copy(out=x1_in[b][:, :, t], in_=g3[:])
+
+        e_banks = [e_pool.tile([P, M], F32, name="e%d" % k) for k in range(4)]
+
+        def second_stage(b):
+            ops = []
+            both = keep.tile([P, 2, M], U32, name="x_codes%d" % b, tag=("gw4", "x_codes1")[b], align_bytes=64)
+            for n, (name, src) in enumerate((("x1", x1_in[b]), ("x2", x2_in[b]))):
+                codes = both[:, n, :]
+                scales = ring.tile([P, M], U8, name=name + "_sc", align_bytes=64)
+                nc.vector.quantize_mx(out=codes.bitcast(FP8X4), scales=scales[:],
+                                      in_=src[:].rearrange("p c t -> p (c t)"))
+                ops.append((codes, scales))
+            (c1, s1), (c2, s2) = ops
+            for k in range(4):
+                nc.tensor.matmul_mx(out=e_banks[k][:], lhsT=c1[:, k * P:(k + 1) * P].bitcast(FP8X4),
+                                    lhsT_scale=s1[:, k * P:(k + 1) * P], rhs=c2.bitcast(FP8X4),
+                                    rhs_scale=s2[:], start=(b == 0), stop=(b == 1))
+
+        staged = first_stage(0)
+        for i in range(NT):
+            ahead = first_stage(i + 1) if i + 1 < NT else None
+            scatter(i, *staged)
+            if i == 0:
+                quantize_w1(1, round_w1(1, w1_raw1))
+            if i == 4:
+                second_stage(0)
+            fetch(i)
+            staged = ahead
+        nc.vector.tensor_copy(out=x1_in[1][:, :, 2:4], in_=x1_last[:].rearrange("p t c -> p c t"))
+        second_stage(1)
+        for k in range(4):
+            res = keep.tile([P, M], F32, name="res%d" % k)
+            nc.vector.tensor_tensor(res[:], e_banks[k][:], fam_sb[:], ALU.add)
+            nc.sync.dma_start(out=out[k * P:(k + 1) * P, :], in_=res[:])

@@ -45,6 +45,7 @@ def tile_list_plating_bath_match_kernel(
         tab_sc = keep.tile([P, T], U8, name="tab_sc", tag="tab_sc", align_bytes=64)
         v_words = {}
         v_sc = keep.tile([P, S], U8, name="v_sc", align_bytes=64)
+        v_sc02 = keep.tile([P, S], U8, name="v_sc02", align_bytes=64)
         v_sc1 = keep.tile([P, S], U8, name="v_sc1", align_bytes=64)
         w4_raw = keep.tile([P, 2, 2 * H], U8, name="w4_raw")
         w4_dealt = keep.tile([P, 2, 2 * H], U8, name="w4_dealt", align_bytes=64)
@@ -54,16 +55,18 @@ def tile_list_plating_bath_match_kernel(
         gain_sb = keep.tile([P, 2, 4], F32, name="gain_sb")
         dv_sb = keep.tile([P, 2, 4], F32, name="dv_sb")
         fam_sb = keep.tile([P, M], F32, name="fam_sb")
-        wg0 = [keep.tile([P, HALF], F32, name="wg0_%d" % h) for h in range(2)]
-        wg1 = keep.tile([P, S], F32, name="wg1")
-        wg23 = keep.tile([P, 2, S], F32, name="wg23")
+        wg = [keep.tile([P, S], F32, name="wg%d" % t) for t in range(4)]
         w1_codes, w1_sc = {}, {}
         x1_in = [keep.tile([P, M, 4], BF16, name="x1_in%d" % b, align_bytes=64) for b in range(2)]
         x2_in = [keep.tile([P, M, 4], BF16, name="x2_in%d" % b, align_bytes=64) for b in range(2)]
-        x1_last = keep.tile([P, 2, M], F32, name="x1_last")
 
-        nc.gpsimd.memset(tab_sc[:].bitcast(I32), 0)
+        for q in range(4):
+            nc.gpsimd.dma_start(out=tab_sc[32 * q + 20:32 * q + 32, :].bitcast(I32),
+                                in_=tab_scales[:, 4 * q:4 * q + 4, :].bitcast(I32))
         nc.vector.memset(w4s_raw[:].rearrange("p a c -> p (a c)").bitcast(I32), 0)
+        for q in range(4):
+            nc.vector.memset(tab_sc[32 * q:32 * q + 20, :].bitcast(I32), 0)
+        nc.vector.memset(v_sc02[:].bitcast(I32), 0)
         nc.vector.memset(v_sc1[:].bitcast(I32), 0)
 
         def load_tab(a):
@@ -82,31 +85,28 @@ def tile_list_plating_bath_match_kernel(
 
         wgs_rows = wgs.rearrange("(x t) j -> x t j", t=4)
 
-        def load_wg0(h):
+        def load_wg(t, lo, hi):
             for u in range(4):
-                nc.sync.dma_start(out=wg0[h][32 * u:32 * u + 32, :], in_=wgs_rows[:, 0, h * HALF:(h + 1) * HALF])
+                nc.sync.dma_start(out=wg[t][32 * u:32 * u + 32, lo:hi], in_=wgs_rows[:, t, lo:hi])
 
-        def load_vec(dst, src):
-            nc.sync.dma_start(out=dst[:], in_=src.rearrange("(b p t) -> p b t", b=2, t=4))
+        def load_vec(dst, src, eng=nc.scalar):
+            eng.dma_start(out=dst[:], in_=src.rearrange("(b p t) -> p b t", b=2, t=4))
 
-        for q in range(4):
-            nc.gpsimd.dma_start(out=tab_sc[32 * q:32 * q + 12, :].bitcast(I32),
-                                in_=tab_scales[:, 4 * q:4 * q + 4, :].bitcast(I32))
-        for q in range(4):
-            nc.gpsimd.dma_start(out=w4s_raw[32 * q:32 * q + 4, :, :].bitcast(I32),
-                                in_=w4_scales[:, 4 * q:4 * q + 4, :].rearrange("a r c -> r a c").bitcast(I32))
         nc.sync.dma_start(idx[:], offs)
         load_tab(0)
+        load_vec(b1_sb, b1)
+        load_vec(gain_sb, gain)
         nc.sync.dma_start(out=w4_raw[:].bitcast(I32), in_=w4_words.rearrange("a p c -> p a c").bitcast(I32))
+        for q in range(4):
+            nc.sync.dma_start(out=w4s_raw[32 * q:32 * q + 4, :, :].bitcast(I32),
+                              in_=w4_scales[:, 4 * q:4 * q + 4, :].rearrange("a r c -> r a c").bitcast(I32))
         w1_raw0 = load_w1(0)
         load_tab(1)
-        load_vec(b1_sb, b1)
+        load_wg(0, 0, HALF)
         load_tab(2)
-        load_vec(gain_sb, gain)
         nc.sync.dma_start(idx2[:], offs2)
-        load_wg0(0)
         page_tiles = [load_page(0)]
-        load_wg0(1)
+        load_wg(0, HALF, S)
 
         def gather_words(a, lo, hi):
             if a not in v_words:
@@ -121,14 +121,15 @@ def tile_list_plating_bath_match_kernel(
             return grouped
 
         def quantize_w1(b, grouped):
-            w1_codes[b] = keep.tile([P, HALF], U32, name="w1_codes%d" % b, tag=("tab1", "w1_codes1")[b], align_bytes=64)
+            w1_codes[b] = keep.tile([P, HALF], U32, name="w1_codes%d" % b, tag=("tab1", "hv_w1")[b], align_bytes=64)
             w1_sc[b] = keep.tile([P, HALF], U8, name="w1_sc%d" % b, tag=("w4s_raw", "w1_sc1")[b], align_bytes=64)
             nc.vector.quantize_mx(out=w1_codes[b][:].bitcast(FP8X4), scales=w1_sc[b][:],
                                   in_=grouped[:].rearrange("p t m j -> p (t m j)"))
 
-        gather_words(0, 0, S)
         nc.vector.tensor_copy(v_sc[:], tab_sc[:].indirect(idx[:]))
-        nc.gpsimd.dma_start(out=v_sc1[0:112, :].bitcast(I32), in_=v_sc[4:116, :].bitcast(I32))
+        nc.scalar.dma_start(out=v_sc02[0:108, :].bitcast(I32), in_=v_sc[20:128, :].bitcast(I32))
+        nc.scalar.dma_start(out=v_sc1[0:104, :].bitcast(I32), in_=v_sc[24:128, :].bitcast(I32))
+        gather_words(0, 0, S)
         nc.vector.tensor_copy(
             out=w4_dealt[:].bitcast(U16).rearrange("p a (b t m) -> p (a b) t m", b=2, t=4),
             in_=w4_raw[:].bitcast(U16).rearrange("p a (b m t) -> p (a b) t m", b=2, t=4))
@@ -140,32 +141,26 @@ def tile_list_plating_bath_match_kernel(
         gather_words(2, 0, HALF)
         gather_words(2, HALF, S)
 
-        w1_raw1 = load_w1(1)
         nc.sync.dma_start(idx4[:], offs4)
         nc.sync.dma_start(idx3[:], offs3)
-        load_vec(dv_sb, dv)
-        for u in range(4):
-            nc.sync.dma_start(out=wg1[32 * u:32 * u + 32, :], in_=wgs_rows[:, 1, :])
-        page_tiles.append(load_page(1))
-        for u in range(4):
-            nc.sync.dma_start(out=wg23[32 * u:32 * u + 32, :, :], in_=wgs_rows[:, 2:4, :])
-        page_tiles.append(load_page(2))
-        page_tiles.append(load_page(3))
-        nc.sync.dma_start(out=fam_sb[:], in_=fam.partition_broadcast(P))
-        for i in range(4, NT):
+        load_vec(dv_sb, dv, nc.sync)
+        for i in range(1, NT):
+            if i < 4:
+                load_wg(i, 0, S)
             page_tiles.append(load_page(i))
+            if i == 1:
+                w1_raw1 = load_w1(1)
+            if i == 4:
+                nc.sync.dma_start(out=fam_sb[:], in_=fam.partition_broadcast(P))
 
         def first_stage(i):
             b, t = divmod(i, 4)
-            th = ring.tile([P, S], F32, name="th")
-            if i == 4:
-                gw = keep.tile([P, S], F32, name="gw4", tag="gw4", align_bytes=64)
-            else:
-                gw = ring.tile([P, S], F32, name="gw")
+            th = keep.tile([P, S], F32, name="th%d" % i, tag="work%d" % (i % 3))
+            hv = keep.tile([P, S], F32, name="hv%d" % i, tag={2: "hv_w1", 5: "hv_x"}.get(i, "hv%d" % (i % 2)), align_bytes=64)
             for h in range(2):
                 cols = slice(h * HALF, (h + 1) * HALF)
-                if t == 0:
-                    nc.scalar.activation(gw[:, cols], wg0[h][:], ACT.Copy, scale=gain_sb[:, b, t:t + 1])
+                if i == 0:
+                    nc.scalar.activation(hv[:, cols], wg[0][:, cols], ACT.Copy, scale=gain_sb[:, b, t:t + 1])
                 acc = acc_pool.tile([P, HALF], F32, name="acc")
                 for a in range(2):
                     nc.tensor.matmul_mx(
@@ -173,57 +168,57 @@ def tile_list_plating_bath_match_kernel(
                         lhsT=w4_dealt[:, a, 2 * P * i:2 * P * (i + 1)].bitcast(FP4X4),
                         lhsT_scale=w4s_dealt[:, a, P * i:P * (i + 1)],
                         rhs=v_words[a][:, cols].bitcast(FP8X4),
-                        rhs_scale=(v_sc, v_sc1)[a][:, cols],
+                        rhs_scale=(v_sc02, v_sc1)[a][:, cols],
                         start=(a == 0), stop=False)
                 nc.tensor.matmul_mx(
                     out=acc[:],
                     lhsT=w1_codes[b][:, P * t:P * (t + 1)].bitcast(FP8X4),
                     lhsT_scale=w1_sc[b][:, P * t:P * (t + 1)],
                     rhs=v_words[2][:, cols].bitcast(FP8X4),
-                    rhs_scale=v_sc[8:P, cols],
+                    rhs_scale=v_sc02[8:P, cols],
                     start=False, stop=True)
                 nc.scalar.activation(th[:, cols], acc[:], ACT.Tanh, bias=b1_sb[:, b, t:t + 1])
-            if t > 0:
-                nc.scalar.activation(gw[:], wg1[:] if t == 1 else wg23[:, t - 2, :], ACT.Copy, scale=gain_sb[:, b, t:t + 1])
-            return th, gw
+            if i == 0:
+                return th, hv
+            nc.scalar.activation(hv[:], th[:], ACT.Copy, scale=gain_sb[:, b, t:t + 1])
+            return hv, wg[t]
 
-        def scatter(i, th, gw):
+        def scatter(i, factors):
             pieces = [(0, HALF), (HALF, S)] if i == 0 else [(0, S)]
             for lo, hi in pieces:
                 nc.vector.tensor_tensor(page_tiles[i][:].indirect(idx2[:, lo // 16:hi // 16]),
-                                        th[:, lo:hi], gw[:, lo:hi], ALU.mult)
+                                        factors[0][:, lo:hi], factors[1][:, lo:hi], ALU.mult)
 
-        def fetch(i):
-            b, t = divmod(i, 4)
+        def fetch(i, g4, g3):
             page = page_tiles[i]
-            g4 = ring.tile([P, M], F32, name="g4")
-            nc.vector.tensor_copy(g4[:], page[:].indirect(idx4[:]))
-            if i >= NT - 2:
-                nc.vector.tensor_copy(x1_last[:, i - (NT - 2), :], page[:].indirect(idx3[:]))
-            else:
-                g3 = ring.tile([P, M], F32, name="g3")
-                nc.vector.tensor_copy(g3[:], page[:].indirect(idx3[:]))
-            if i == 0:
-                mag = keep.tile([P, M], F32, name="mag0", tag="w1_raw1")
-            else:
-                mag = ring.tile([P, M], F32, name="mag")
-            nc.scalar.activation(mag[:], g4[:], ACT.Abs)
+            nc.vector.tensor_copy(g4, page[:].indirect(idx4[:]))
+            nc.vector.tensor_copy(g3, page[:].indirect(idx3[:]))
+
+        def weave_x2(i, g4):
+            b, t = divmod(i, 4)
+            mag = ring.tile([P, M], F32, name="mag")
+            nc.scalar.activation(mag[:], g4, ACT.Abs)
             nc.scalar.activation(x2_in[b][:, :, t], mag[:], ACT.Copy, scale=dv_sb[:, b, t:t + 1])
-            if i < NT - 2:
-                nc.scalar.copy(out=x1_in[b][:, :, t], in_=g3[:])
+
+        def fetch_and_weave(i):
+            b, t = divmod(i, 4)
+            got = keep.tile([P, 2, M], F32, name="got%d" % i, tag="work%d" % ((i + 1) % 3))
+            fetch(i, got[:, 0, :], got[:, 1, :])
+            weave_x2(i, got[:, 0, :])
+            nc.scalar.copy(out=x1_in[b][:, :, t], in_=got[:, 1, :])
 
         e_banks = [e_pool.tile([P, M], F32, name="e%d" % k) for k in range(4)]
 
         def second_stage(b):
-            ops = []
-            both = keep.tile([P, 2, M], U32, name="x_codes%d" % b, tag=("gw4", "x_codes1")[b], align_bytes=64)
-            for n, (name, src) in enumerate((("x1", x1_in[b]), ("x2", x2_in[b]))):
-                codes = both[:, n, :]
-                scales = ring.tile([P, M], U8, name=name + "_sc", align_bytes=64)
-                nc.vector.quantize_mx(out=codes.bitcast(FP8X4), scales=scales[:],
-                                      in_=src[:].rearrange("p c t -> p (c t)"))
-                ops.append((codes, scales))
-            (c1, s1), (c2, s2) = ops
+            codes = keep.tile([P, 2, M], U32, name="x_codes%d" % b, tag=("hv_x", "x_codes1")[b], align_bytes=64)
+            s1 = ring.tile([P, M], U8, name="x1_sc", align_bytes=64)
+            s2 = ring.tile([P, M], U8, name="x2_sc", align_bytes=64)
+            c1, c2 = codes[:, 0, :], codes[:, 1, :]
+            nc.vector.quantize_mx(out=c2.bitcast(FP8X4), scales=s2[:], in_=x2_in[b][:].rearrange("p c t -> p (c t)"))
+            for lo in (0, M // 2):
+                cols = slice(lo, lo + M // 2)
+                nc.vector.quantize_mx(out=c1[:, cols].bitcast(FP8X4), scales=s1[:, cols],
+                                      in_=x1_in[b][:, cols, :].rearrange("p c t -> p (c t)"))
             for k in range(4):
                 nc.tensor.matmul_mx(out=e_banks[k][:], lhsT=c1[:, k * P:(k + 1) * P].bitcast(FP8X4),
                                     lhsT_scale=s1[:, k * P:(k + 1) * P], rhs=c2.bitcast(FP8X4),
@@ -232,14 +227,19 @@ def tile_list_plating_bath_match_kernel(
         staged = first_stage(0)
         for i in range(NT):
             ahead = first_stage(i + 1) if i + 1 < NT else None
-            scatter(i, *staged)
-            if i == 0:
+            scatter(i, staged)
+            if i == 2:
                 quantize_w1(1, round_w1(1, w1_raw1))
-            if i == 4:
+            if i == 5:
                 second_stage(0)
-            fetch(i)
+            if 1 <= i < NT - 1:
+                fetch_and_weave(i - 1)
             staged = ahead
-        nc.vector.tensor_copy(out=x1_in[1][:, :, 2:4], in_=x1_last[:].rearrange("p t c -> p c t"))
+        last = keep.tile([P, 2, 2, M], F32, name="last", tag="work%d" % ((NT - 1) % 3))
+        for n in range(2):
+            fetch(NT - 2 + n, last[:, 0, n, :], last[:, 1, n, :])
+            weave_x2(NT - 2 + n, last[:, 0, n, :])
+        nc.vector.tensor_copy(out=x1_in[1][:, :, 2:4], in_=last[:, 1, :, :].rearrange("p t c -> p c t"))
         second_stage(1)
         for k in range(4):
             res = keep.tile([P, M], F32, name="res%d" % k)

from contextlib import ExitStack

import concourse.mybir as mybir

FLOPS = 3758096384

F32 = mybir.dt.float32
BF16 = mybir.dt.bfloat16
I32 = mybir.dt.int32
U32 = mybir.dt.uint32
U16 = mybir.dt.uint16
U8 = mybir.dt.uint8
FP8X4 = mybir.dt.float8_e4m3fn_x4
FP4X4 = mybir.dt.float4_e2m1fn_x4
ACT = mybir.ActivationFunctionType
ALU = mybir.AluOpType

P = 128
T = 4096
S = 1024
T2 = 2048
M = 512
H = 1024
HALF = 512
NT = 8


def tile_list_plating_bath_match_kernel(
    tc, tab_words, tab_scales, offs, offs2, offs3, offs4, w4_words, w4_scales,
    w1, b1, gain, wgs, page0, dv, fam, out,
):
    nc = tc.nc
    with ExitStack() as ctx:
        keep = ctx.enter_context(tc.tile_pool(name="keep", bufs=1))
        ring = ctx.enter_context(tc.tile_pool(name="ring", bufs=2))
        pages = ctx.enter_context(tc.tile_pool(name="pages", bufs=5))
        acc_pool = ctx.enter_context(tc.psum_pool(name="acc", bufs=4))
        e_pool = ctx.enter_context(tc.psum_pool(name="e", bufs=1))

        idx = keep.tile([P, S // 16], U16, name="idx")
        idx2 = keep.tile([P, S // 16], U16, name="idx2")
        idx3 = keep.tile([P, M // 16], U16, name="idx3")
        idx4 = keep.tile([P, M // 16], U16, name="idx4")
        tab = [keep.tile([P, T], I32, name="tab%d" % a, tag="tab%d" % a, align_bytes=64) for a in range(3)]
        tab_sc = keep.tile([P, T], U8, name="tab_sc", tag="tab_sc", align_bytes=64)
        v_words = {}
        v_sc = keep.tile([P, S], U8, name="v_sc", align_bytes=64)
        v_sc02 = keep.tile([P, S], U8, name="v_sc02", align_bytes=64)
        v_sc1 = keep.tile([P, S], U8, name="v_sc1", align_bytes=64)
        w4_raw = keep.tile([P, 2, 2 * H], U8, name="w4_raw")
        w4_dealt = keep.tile([P, 2, 2 * H], U8, name="w4_dealt", align_bytes=64)
        w4s_raw = keep.tile([P, 2, H], U8, name="w4s_raw", tag="w4s_raw", align_bytes=64)
        w4s_dealt = keep.tile([P, 2, H], U8, name="w4s_dealt", align_bytes=64)
        b1_sb = keep.tile([P, 2, 4], F32, name="b1_sb")
        gain_sb = keep.tile([P, 2, 4], F32, name="gain_sb")
        dv_sb = keep.tile([P, 2, 4], F32, name="dv_sb")
        fam_sb = keep.tile([P, M], F32, name="fam_sb")
        wg = [keep.tile([P, S], F32, name="wg%d" % t) for t in range(4)]
        w1_codes, w1_sc = {}, {}
        x1_in = [keep.tile([P, M, 4], BF16, name="x1_in%d" % b, align_bytes=64) for b in range(2)]
        x2_in = [keep.tile([P, M, 4], BF16, name="x2_in%d" % b, align_bytes=64) for b in range(2)]

        for q in range(4):
            nc.gpsimd.dma_start(out=tab_sc[32 * q + 20:32 * q + 32, :].bitcast(I32),
                                in_=tab_scales[:, 4 * q:4 * q + 4, :].bitcast(I32))
        nc.vector.memset(w4s_raw[:].rearrange("p a c -> p (a c)").bitcast(I32), 0)
        for q in range(4):
            nc.vector.memset(tab_sc[32 * q:32 * q + 20, :].bitcast(I32), 0)
        nc.vector.memset(v_sc02[:].bitcast(I32), 0)
        nc.vector.memset(v_sc1[:].bitcast(I32), 0)

        def load_tab(a):
            nc.sync.dma_start(out=tab[a][:], in_=tab_words[a].rearrange("p n t -> p (n t)").bitcast(I32))

        def load_w1(b):
            raw = keep.tile([P, 4, HALF], F32, name="w1_raw%d" % b, tag="w1_raw%d" % b)
            nc.sync.dma_start(out=raw[:], in_=w1[:, b * HALF:(b + 1) * HALF].rearrange("(p j) c -> p j c", j=4))
            return raw

        def load_page(i):
            b, t = divmod(i, 4)
            page = pages.tile([P, T2], F32, name="page")
            nc.sync.dma_start(out=page[:], in_=page0[b * HALF:(b + 1) * HALF, :].rearrange("(p t) c -> t p c", t=4)[t])
            return page

        wgs_rows = wgs.rearrange("(x t) j -> x t j", t=4)

        def load_wg(t, lo, hi):
            for u in range(4):
                nc.sync.dma_start(out=wg[t][32 * u:32 * u + 32, lo:hi], in_=wgs_rows[:, t, lo:hi])

        def load_vec(dst, src, eng=nc.scalar):
            eng.dma_start(out=dst[:], in_=src.rearrange("(b p t) -> p b t", b=2, t=4))

        nc.sync.dma_start(idx[:], offs)
        load_tab(0)
        load_vec(b1_sb, b1)
        load_vec(gain_sb, gain)
        nc.sync.dma_start(out=w4_raw[:].bitcast(I32), in_=w4_words.rearrange("a p c -> p a c").bitcast(I32))
        for q in range(4):
            nc.sync.dma_start(out=w4s_raw[32 * q:32 * q + 4, :, :].bitcast(I32),
                              in_=w4_scales[:, 4 * q:4 * q + 4, :].rearrange("a r c -> r a c").bitcast(I32))
        w1_raw0 = load_w1(0)
        load_tab(1)
        load_wg(0, 0, HALF)
        load_tab(2)
        nc.sync.dma_start(idx2[:], offs2)
        page_tiles = [load_page(0)]
        load_wg(0, HALF, S)

        def gather_words(a, lo, hi):
            if a not in v_words:
                v_words[a] = keep.tile([P, S], U32, name="v_words%d" % a, align_bytes=64,
                                       tag=("v_words0", "tab_sc", "w1_grouped0")[a])
            nc.vector.tensor_copy(v_words[a][:, lo:hi], tab[a][:].bitcast(U32).indirect(idx[:, lo // 16:hi // 16]))

        def round_w1(b, raw):
            grouped = keep.tile([P, 4, P, 4], BF16, name="w1_grouped%d" % b, tag="w1_grouped%d" % b, align_bytes=64)
            nc.scalar.copy(out=grouped[:].rearrange("p t m j -> p m t j"),
                           in_=raw[:].rearrange("p j (m t) -> p m t j", t=4))
            return grouped

        def quantize_w1(b, grouped):
            w1_codes[b] = keep.tile([P, HALF], U32, name="w1_codes%d" % b, tag=("tab1", "hv_w1")[b], align_bytes=64)
            w1_sc[b] = keep.tile([P, HALF], U8, name="w1_sc%d" % b, tag=("w4s_raw", "w1_sc1")[b], align_bytes=64)
            nc.vector.quantize_mx(out=w1_codes[b][:].bitcast(FP8X4), scales=w1_sc[b][:],
                                  in_=grouped[:].rearrange("p t m j -> p (t m j)"))

        nc.vector.tensor_copy(v_sc[:], tab_sc[:].indirect(idx[:]))
        nc.scalar.dma_start(out=v_sc02[0:108, :].bitcast(I32), in_=v_sc[20:128, :].bitcast(I32))
        nc.scalar.dma_start(out=v_sc1[0:104, :].bitcast(I32), in_=v_sc[24:128, :].bitcast(I32))
        gather_words(0, 0, S)
        nc.vector.tensor_copy(
            out=w4_dealt[:].bitcast(U16).rearrange("p a (b t m) -> p (a b) t m", b=2, t=4),
            in_=w4_raw[:].bitcast(U16).rearrange("p a (b m t) -> p (a b) t m", b=2, t=4))
        nc.vector.tensor_copy(
            out=w4s_dealt[:].rearrange("p a (b t m) -> p (a b) t m", b=2, t=4),
            in_=w4s_raw[:].rearrange("p a (b m t) -> p (a b) t m", b=2, t=4))
        gather_words(1, 0, S)
        quantize_w1(0, round_w1(0, w1_raw0))
        gather_words(2, 0, HALF)
        gather_words(2, HALF, S)

        nc.sync.dma_start(idx4[:], offs4)
        nc.sync.dma_start(idx3[:], offs3)
        load_vec(dv_sb, dv, nc.sync)
        for i in range(1, NT):
            if i < 4:
                load_wg(i, 0, S)
            page_tiles.append(load_page(i))
            if i == 1:
                w1_raw1 = load_w1(1)
            if i == 4:
                nc.sync.dma_start(out=fam_sb[:], in_=fam.partition_broadcast(P))

        def first_stage(i):
            b, t = divmod(i, 4)
            th = keep.tile([P, S], F32, name="th%d" % i, tag="work%d" % (i % 3))
            hv = keep.tile([P, S], F32, name="hv%d" % i, tag={2: "hv_w1", 5: "hv_x"}.get(i, "hv%d" % (i % 2)), align_bytes=64)
            for h in range(2):
                cols = slice(h * HALF, (h + 1) * HALF)
                if i == 0:
                    nc.scalar.activation(hv[:, cols], wg[0][:, cols], ACT.Copy, scale=gain_sb[:, b, t:t + 1])
                acc = acc_pool.tile([P, HALF], F32, name="acc")
                for a in range(2):
                    nc.tensor.matmul_mx(
                        out=acc[:],
                        lhsT=w4_dealt[:, a, 2 * P * i:2 * P * (i + 1)].bitcast(FP4X4),
                        lhsT_scale=w4s_dealt[:, a, P * i:P * (i + 1)],
                        rhs=v_words[a][:, cols].bitcast(FP8X4),
                        rhs_scale=(v_sc02, v_sc1)[a][:, cols],
                        start=(a == 0), stop=False)
                nc.tensor.matmul_mx(
                    out=acc[:],
                    lhsT=w1_codes[b][:, P * t:P * (t + 1)].bitcast(FP8X4),
                    lhsT_scale=w1_sc[b][:, P * t:P * (t + 1)],
                    rhs=v_words[2][:, cols].bitcast(FP8X4),
                    rhs_scale=v_sc02[8:P, cols],
                    start=False, stop=True)
                nc.scalar.activation(th[:, cols], acc[:], ACT.Tanh, bias=b1_sb[:, b, t:t + 1])
            if i == 0:
                return th, hv
            nc.scalar.activation(hv[:], th[:], ACT.Copy, scale=gain_sb[:, b, t:t + 1])
            return hv, wg[t]

        def scatter(i, factors):
            pieces = [(0, HALF), (HALF, S)] if i == 0 else [(0, S)]
            for lo, hi in pieces:
                nc.vector.tensor_tensor(page_tiles[i][:].indirect(idx2[:, lo // 16:hi // 16]),
                                        factors[0][:, lo:hi], factors[1][:, lo:hi], ALU.mult)

        def fetch(i, g4, g3):
            page = page_tiles[i]
            nc.vector.tensor_copy(g4, page[:].indirect(idx4[:]))
            nc.vector.tensor_copy(g3, page[:].indirect(idx3[:]))

        def weave_x2(i, g4):
            b, t = divmod(i, 4)
            mag = ring.tile([P, M], F32, name="mag")
            nc.scalar.activation(mag[:], g4, ACT.Abs)
            nc.scalar.activation(x2_in[b][:, :, t], mag[:], ACT.Copy, scale=dv_sb[:, b, t:t + 1])

        def fetch_and_weave(i):
            b, t = divmod(i, 4)
            got = keep.tile([P, 2, M], F32, name="got%d" % i, tag="work%d" % ((i + 1) % 3))
            fetch(i, got[:, 0, :], got[:, 1, :])
            weave_x2(i, got[:, 0, :])
            nc.scalar.copy(out=x1_in[b][:, :, t], in_=got[:, 1, :])

        e_banks = [e_pool.tile([P, M], F32, name="e%d" % k) for k in range(4)]

        def second_stage(b):
            codes = keep.tile([P, 2, M], U32, name="x_codes%d" % b, tag=("hv_x", "x_codes1")[b], align_bytes=64)
            s1 = ring.tile([P, M], U8, name="x1_sc", align_bytes=64)
            s2 = ring.tile([P, M], U8, name="x2_sc", align_bytes=64)
            c1, c2 = codes[:, 0, :], codes[:, 1, :]
            nc.vector.quantize_mx(out=c2.bitcast(FP8X4), scales=s2[:], in_=x2_in[b][:].rearrange("p c t -> p (c t)"))
            for lo in (0, M // 2):
                cols = slice(lo, lo + M // 2)
                nc.vector.quantize_mx(out=c1[:, cols].bitcast(FP8X4), scales=s1[:, cols],
                                      in_=x1_in[b][:, cols, :].rearrange("p c t -> p (c t)"))
            for k in range(4):
                nc.tensor.matmul_mx(out=e_banks[k][:], lhsT=c1[:, k * P:(k + 1) * P].bitcast(FP8X4),
                                    lhsT_scale=s1[:, k * P:(k + 1) * P], rhs=c2.bitcast(FP8X4),
                                    rhs_scale=s2[:], start=(b == 0), stop=(b == 1))

        staged = first_stage(0)
        for i in range(NT):
            ahead = first_stage(i + 1) if i + 1 < NT else None
            scatter(i, staged)
            if i == 2:
                quantize_w1(1, round_w1(1, w1_raw1))
            if i == 5:
                second_stage(0)
            if 1 <= i < NT - 1:
                fetch_and_weave(i - 1)
            staged = ahead
        last = keep.tile([P, 2, 2, M], F32, name="last", tag="work%d" % ((NT - 1) % 3))
        for n in range(2):
            fetch(NT - 2 + n, last[:, 0, n, :], last[:, 1, n, :])
            weave_x2(NT - 2 + n, last[:, 0, n, :])
        nc.vector.tensor_copy(out=x1_in[1][:, :, 2:4], in_=last[:, 1, :, :].rearrange("p t c -> p c t"))
        second_stage(1)
        for k in range(4):
            res = keep.tile([P, M], F32, name="res%d" % k)
            nc.vector.tensor_tensor(res[:], e_banks[k][:], fam_sb[:], ALU.add)
            nc.sync.dma_start(out=out[k * P:(k + 1) * P, :], in_=res[:])
